import numpy as np
import ml_dtypes


def mxq(x, axis, fmt="e4m3"):
    dtype, down = {"e4m3": (ml_dtypes.float8_e4m3fn, 7), "e5m2": (ml_dtypes.float8_e5m2, 14)}[fmt]
    v = np.moveaxis(np.asarray(x, np.float32).astype(ml_dtypes.bfloat16).astype(np.float64), axis, -1)
    blocks = v.reshape(v.shape[:-1] + (-1, 32))
    amax = np.abs(blocks).max(-1, keepdims=True)
    byte = np.maximum(np.where(amax > 0, np.frexp(amax)[1] - 1 + 127, 0) - down, 1)
    scale = np.exp2(byte - 127.0)
    codes = (blocks / scale).astype(np.float32).astype(dtype).astype(np.float64)
    return np.moveaxis((codes * scale).reshape(v.shape), -1, axis)


WIDE = False


def mx_kscale(k):
    if not WIDE:
        return np.ones(k)
    levels = np.array([10, -10, 5, -5, 0])
    if k % 512:
        return np.exp2(np.random.permutation(np.resize(levels, k // 32))).repeat(32)
    a = np.empty((k // 512, 16))
    for p in range(k // 512):
        a[p, :8] = np.random.permutation(np.resize(levels, 8))
        for g in range(8):
            far = levels[np.abs(levels - a[p, g]) >= 10]
            a[p, g + 8] = far[np.random.randint(len(far))]
    return np.exp2(a.ravel()).repeat(32)


def f64(x):
    return np.asarray(x).astype(np.float64)


def striped(idx):
    return np.tile(np.asarray(idx).reshape(-1, 16).T, (8, 1)).astype(np.uint16)


def unstriped(offs):
    return offs[:16].T.reshape(-1).astype(np.int64)


E2M1 = np.array([0.0, 0.5, 1.0, 1.5, 2.0, 3.0, 4.0, 6.0, -0.0, -0.5, -1.0, -1.5, -2.0, -3.0, -4.0, -6.0])


def pack_weight(w, fmt):
    k, n = w.shape
    w = f64(np.asarray(w, np.float32).astype(ml_dtypes.bfloat16)).reshape(k // 32, 32, n)
    amax = np.abs(w).max(1)
    if fmt == "e4m3":
        byte = np.frexp(amax)[1] - 1 + 127 - 7
    else:
        mant, ex = np.frexp(amax / 6.0)
        byte = np.where(mant > 0.5, ex, ex - 1) + 127
    byte = np.clip(np.where(amax > 0, byte, 1), 1, 254)
    scaled = (w * np.exp2(127.0 - byte)[:, None, :]).reshape(k, n).astype(np.float32)
    by_word = np.ascontiguousarray(scaled.reshape(k // 512, 128, 4, n).transpose(0, 1, 3, 2))
    if fmt == "e4m3":
        words = by_word.astype(ml_dtypes.float8_e4m3fn).view(np.uint8)
    else:
        c = by_word.astype(ml_dtypes.float4_e2m1fn).view(np.uint8) & 0xF
        words = (c[..., 0::2] | (c[..., 1::2] << 4)).reshape(k // 512, 128, 2 * n)
    return np.ascontiguousarray(words), np.ascontiguousarray(byte.astype(np.uint8).reshape(k // 512, 16, n))


def unpack_weight(words, scales, fmt):
    g, _, n = scales.shape
    words = np.ascontiguousarray(words).reshape(g, 128, n, -1)
    if fmt == "e4m3":
        vals = words.view(ml_dtypes.float8_e4m3fn).astype(np.float64)
    else:
        nib = np.empty((g, 128, n, 4), np.uint8)
        nib[..., 0::2] = words & 0xF
        nib[..., 1::2] = words >> 4
        vals = E2M1[nib]
    vals = vals * np.repeat(np.exp2(scales.astype(np.float64) - 127.0), 8, axis=1)[..., None]
    return vals.transpose(0, 1, 3, 2).reshape(g * 512, n)


K, T, J, N = 512, 512, 512, 512


def setup_inputs():
    n = np.random.standard_normal
    idx = np.random.randint(0, T, J)
    idx2 = np.random.randint(0, T, J)
    fk = mx_kscale(K)
    xtp = pack_weight(n((K, T)) / fk[:, None], "e4m3")
    wap = pack_weight(n((K, N)) * 1 / np.sqrt(K) * fk[:, None], "e2m1")
    return {
        "xt_words": xtp[0],
        "xt_scales": xtp[1],
        "wa_words": wap[0],
        "wa_scales": wap[1],
        "wb": (n((K, N)) * 1 / np.sqrt(K) * fk[:, None]).astype(np.float32),
        "offs": striped(idx),
        "offs2": striped(idx2),
    }


def reference(xt_words, xt_scales, wa_words, wa_scales, wb, offs, offs2):
    idx = unstriped(offs)
    idx2 = unstriped(offs2)
    xtu = unpack_weight(xt_words, xt_scales, "e4m3")
    wau = unpack_weight(wa_words, wa_scales, "e2m1")
    za = wau.T @ xtu
    wbq = mxq(f64(wb), 0, "e4m3")
    zb = wbq.T @ xtu
    y = za[:, idx] * zb[:, idx2] - za[:, idx2] * zb[:, idx]
    return y

@@ -1,0 +1,147 @@
+from contextlib import ExitStack
+
+import concourse.mybir as mybir
+
+K, T, J, N = 512, 512, 512, 512
+FLOPS = 2 * 2 * K * N * T
+
+F32 = mybir.dt.float32
+BF16 = mybir.dt.bfloat16
+I32 = mybir.dt.int32
+U32 = mybir.dt.uint32
+U16 = mybir.dt.uint16
+U8 = mybir.dt.uint8
+FP8X4 = mybir.dt.float8_e4m3fn_x4
+FP4X4 = mybir.dt.float4_e2m1fn_x4
+COPY = mybir.ActivationFunctionType.Copy
+MULT = mybir.AluOpType.mult
+SUBTRACT = mybir.AluOpType.subtract
+
+P = 128
+PACK = 4
+BLOCKS = N // P
+SPARE = 16
+VECTOR_EMPTIES = 2
+PIECES = [(0, 0, 256), (0, 256, 512), (1, 0, 512), (2, 0, 512), (3, 0, 256), (3, 256, 512)]
+
+
+def tile_list_antisymmetric_pair_kernel(tc, xt_words, xt_scales, wa_words, wa_scales, wb, offs, offs2, out):
+    nc = tc.nc
+    with ExitStack() as ctx:
+        lists = ctx.enter_context(tc.tile_pool(name="lists", bufs=1))
+        keep = ctx.enter_context(tc.tile_pool(name="keep", bufs=1))
+        psum = ctx.enter_context(tc.psum_pool(name="psum", bufs=1))
+
+        first = lists.tile([P, J // 16], U16, name="first")
+        second = lists.tile([P, J // 16], U16, name="second")
+        x_codes = keep.tile([P, T], U32, name="x_codes", align_bytes=64)
+        x_scale = keep.tile([P, T], U8, name="x_scale", align_bytes=64)
+        a_codes = keep.tile([P, 2 * N], U8, name="a_codes", align_bytes=64)
+        a_scale = keep.tile([P, N], U8, name="a_scale", align_bytes=64)
+        b_raw = [keep.tile([P, PACK, P], F32, name="b_raw%d" % c) for c in range(BLOCKS)]
+        b_grouped = [keep.tile([P, P, PACK], BF16, name="b_grouped%d" % c, align_bytes=64) for c in range(BLOCKS)]
+        b_codes = [keep.tile([P, P], U32, name="b_codes%d" % c, align_bytes=64) for c in range(BLOCKS)]
+        b_scale = [keep.tile([P, P], U8, name="b_scale%d" % c, align_bytes=64) for c in range(BLOCKS)]
+        za = [keep.tile([P, T + SPARE], F32, name="za%d" % c) for c in range(BLOCKS)]
+        zb = [keep.tile([P, T + SPARE], F32, name="zb%d" % c) for c in range(BLOCKS)]
+        a_bank = [psum.tile([P, T], F32, name="a_bank%d" % c) for c in range(BLOCKS)]
+        b_bank = [psum.tile([P, T], F32, name="b_bank%d" % c) for c in range(BLOCKS)]
+
+        def load_scale_rows(queue, plane, rows, q):
+            queue.dma_start(out=plane[32 * q : 32 * q + 4, :].bitcast(I32), in_=rows[0, 4 * q : 4 * q + 4, :].bitcast(I32))
+
+        wb_rows = wb.rearrange("(p j) n -> p j n", j=PACK)
+
+        def load_wb(queue, c):
+            queue.dma_start(out=b_raw[c][:], in_=wb_rows[:, :, P * c : P * (c + 1)])
+
+        for q in range(4):
+            load_scale_rows(nc.sync, x_scale, xt_scales, q)
+        load_scale_rows(nc.sync, a_scale, wa_scales, 0)
+        load_wb(nc.sync, 0)
+        nc.sync.dma_start(out=x_codes[:].bitcast(I32), in_=xt_words[0].rearrange("p t r -> p (t r)").bitcast(I32))
+        nc.sync.dma_start(out=a_codes[:].bitcast(I32), in_=wa_words[0].bitcast(I32))
+        for q in range(1, 4):
+            load_scale_rows(nc.sync, a_scale, wa_scales, q)
+        nc.sync.dma_start(first[:], offs)
+        nc.sync.dma_start(second[:], offs2)
+        for c in range(1, BLOCKS):
+            load_wb(nc.sync, c)
+
+        def multiply_a(c):
+            nc.tensor.matmul_mx(
+                out=a_bank[c][:],
+                lhsT=a_codes[:, 2 * P * c : 2 * P * (c + 1)].bitcast(FP4X4),
+                lhsT_scale=a_scale[:, P * c : P * (c + 1)],
+                rhs=x_codes[:].bitcast(FP8X4),
+                rhs_scale=x_scale[:],
+                start=True,
+                stop=True,
+            )
+
+        def round_b(c):
+            nc.vector.tensor_copy(
+                out=b_grouped[c][:].rearrange("p (c i) j -> p c j i", i=4),
+                in_=b_raw[c][:].rearrange("p j (c i) -> p c j i", i=4),
+            )
+
+        def quantise_b(c):
+            nc.vector.quantize_mx(
+                out=b_codes[c][:].bitcast(FP8X4),
+                scales=b_scale[c][:],
+                in_=b_grouped[c][:].rearrange("p n j -> p (n j)"),
+            )
+
+        def multiply_b(c):
+            nc.tensor.matmul_mx(
+                out=b_bank[c][:],
+                lhsT=b_codes[c][:].bitcast(FP8X4),
+                lhsT_scale=b_scale[c][:],
+                rhs=x_codes[:].bitcast(FP8X4),
+                rhs_scale=x_scale[:],
+                start=True,
+                stop=True,
+            )
+
+        def empty_banks(c):
+            nc.scalar.copy(out=za[c][:, 0:T], in_=a_bank[c][:])
+            if c < VECTOR_EMPTIES:
+                nc.vector.tensor_copy(out=zb[c][:, 0:T], in_=b_bank[c][:])
+            else:
+                nc.scalar.copy(out=zb[c][:, 0:T], in_=b_bank[c][:])
+
+        def products(u):
+            c, lo, hi = PIECES[u]
+            width = hi - lo
+            first_part, second_part = first[:, lo // 16 : hi // 16], second[:, lo // 16 : hi // 16]
+            za_first = keep.tile([P, width], F32, name="za_first%d" % u)
+            za_second = keep.tile([P, width], F32, name="za_second%d" % u)
+            direct = keep.tile([P, width], F32, name="direct%d" % u)
+            swapped = keep.tile([P, width], F32, name="swapped%d" % u)
+            nc.scalar.activation(za_first[:], za[c][:].indirect(first_part), COPY)
+            nc.scalar.activation(za_second[:], za[c][:].indirect(second_part), COPY)
+            nc.vector.tensor_tensor(direct[:], zb[c][:].indirect(second_part), za_first[:], MULT)
+            if u > 0:
+                finish(u - 1)
+            nc.vector.tensor_tensor(swapped[:], zb[c][:].indirect(first_part), za_second[:], MULT)
+            made.append((direct, swapped))
+
+        def finish(u):
+            c, lo, hi = PIECES[u]
+            direct, swapped = made[u]
+            result = keep.tile([P, hi - lo], F32, name="result%d" % u)
+            nc.vector.tensor_tensor(result[:], direct[:], swapped[:], SUBTRACT)
+            nc.sync.dma_start(out=out[P * c : P * (c + 1), lo:hi], in_=result[:])
+
+        made = []
+        for c in range(BLOCKS):
+            round_b(c)
+            quantise_b(c)
+            multiply_a(c)
+            multiply_b(c)
+        for c in range(BLOCKS):
+            empty_banks(c)
+            for u in range(len(PIECES)):
+                if PIECES[u][0] == c:
+                    products(u)
+        finish(len(PIECES) - 1)

@@ -21,8 +21,10 @@ P = 128
 PACK = 4
 BLOCKS = N // P
 SPARE = 16
-VECTOR_EMPTIES = 2
-PIECES = [(0, 0, 256), (0, 256, 512), (1, 0, 512), (2, 0, 512), (3, 0, 256), (3, 256, 512)]
+WB_LOADS = [(0, 1), (1, 2), (2, 4)]
+HEAD_CUT = 256
+TAIL_CUT = 320
+ALL = slice(0, J)
 
 
 def tile_list_antisymmetric_pair_kernel(tc, xt_words, xt_scales, wa_words, wa_scales, wb, offs, offs2, out):
@@ -32,43 +34,45 @@ def tile_list_antisymmetric_pair_kernel(tc, xt_words, xt_scales, wa_words, wa_sc
         keep = ctx.enter_context(tc.tile_pool(name="keep", bufs=1))
         psum = ctx.enter_context(tc.psum_pool(name="psum", bufs=1))
 
+        def sbuf(shape, dtype, name, after=None):
+            return keep.tile(shape, dtype, name=name, tag=after or name, align_bytes=64)
+
         first = lists.tile([P, J // 16], U16, name="first")
         second = lists.tile([P, J // 16], U16, name="second")
-        x_codes = keep.tile([P, T], U32, name="x_codes", align_bytes=64)
-        x_scale = keep.tile([P, T], U8, name="x_scale", align_bytes=64)
-        a_codes = keep.tile([P, 2 * N], U8, name="a_codes", align_bytes=64)
-        a_scale = keep.tile([P, N], U8, name="a_scale", align_bytes=64)
-        b_raw = [keep.tile([P, PACK, P], F32, name="b_raw%d" % c) for c in range(BLOCKS)]
-        b_grouped = [keep.tile([P, P, PACK], BF16, name="b_grouped%d" % c, align_bytes=64) for c in range(BLOCKS)]
-        b_codes = [keep.tile([P, P], U32, name="b_codes%d" % c, align_bytes=64) for c in range(BLOCKS)]
-        b_scale = [keep.tile([P, P], U8, name="b_scale%d" % c, align_bytes=64) for c in range(BLOCKS)]
-        za = [keep.tile([P, T + SPARE], F32, name="za%d" % c) for c in range(BLOCKS)]
-        zb = [keep.tile([P, T + SPARE], F32, name="zb%d" % c) for c in range(BLOCKS)]
-        a_bank = [psum.tile([P, T], F32, name="a_bank%d" % c) for c in range(BLOCKS)]
-        b_bank = [psum.tile([P, T], F32, name="b_bank%d" % c) for c in range(BLOCKS)]
+        x_codes = sbuf([P, T], U32, "x_codes")
+        x_scale = sbuf([P, T], U8, "x_scale")
+        a_codes = sbuf([P, 2 * N], U8, "a_codes")
+        a_scale = sbuf([P, N], U8, "a_scale")
+        widths = [P * (hi - lo) for lo, hi in WB_LOADS]
+        b_raw = [sbuf([P, PACK, w], F32, "b_raw%d" % h) for h, w in enumerate(widths)]
+        b_grouped = [sbuf([P, w, PACK], BF16, "b_grouped%d" % h) for h, w in enumerate(widths)]
+        b_codes = [sbuf([P, w], U32, "b_codes%d" % h) for h, w in enumerate(widths)]
+        b_scale = [sbuf([P, w], U8, "b_scale%d" % h) for h, w in enumerate(widths)]
 
-        def load_scale_rows(queue, plane, rows, q):
-            queue.dma_start(out=plane[32 * q : 32 * q + 4, :].bitcast(I32), in_=rows[0, 4 * q : 4 * q + 4, :].bitcast(I32))
+        def load_scales(plane, rows):
+            for q in range(4):
+                nc.sync.dma_start(out=plane[32 * q : 32 * q + 4, :].bitcast(I32), in_=rows[0, 4 * q : 4 * q + 4, :].bitcast(I32))
 
         wb_rows = wb.rearrange("(p j) n -> p j n", j=PACK)
 
-        def load_wb(queue, c):
-            queue.dma_start(out=b_raw[c][:], in_=wb_rows[:, :, P * c : P * (c + 1)])
+        def load_wb(h):
+            lo, hi = WB_LOADS[h]
+            nc.sync.dma_start(out=b_raw[h][:], in_=wb_rows[:, :, P * lo : P * hi])
 
-        for q in range(4):
-            load_scale_rows(nc.sync, x_scale, xt_scales, q)
-        load_scale_rows(nc.sync, a_scale, wa_scales, 0)
-        load_wb(nc.sync, 0)
+        load_scales(x_scale, xt_scales)
+        load_wb(0)
         nc.sync.dma_start(out=x_codes[:].bitcast(I32), in_=xt_words[0].rearrange("p t r -> p (t r)").bitcast(I32))
         nc.sync.dma_start(out=a_codes[:].bitcast(I32), in_=wa_words[0].bitcast(I32))
-        for q in range(1, 4):
-            load_scale_rows(nc.sync, a_scale, wa_scales, q)
-        nc.sync.dma_start(first[:], offs)
+        load_wb(1)
+        load_scales(a_scale, wa_scales)
         nc.sync.dma_start(second[:], offs2)
-        for c in range(1, BLOCKS):
-            load_wb(nc.sync, c)
+        nc.sync.dma_start(first[:], offs)
+        load_wb(2)
+
+        a_bank, b_bank, za, zb, direct, swapped, result = {}, {}, {}, {}, {}, {}, {}
 
         def multiply_a(c):
+            a_bank[c] = psum.tile([P, T], F32, name="a_bank%d" % c)
             nc.tensor.matmul_mx(
                 out=a_bank[c][:],
                 lhsT=a_codes[:, 2 * P * c : 2 * P * (c + 1)].bitcast(FP4X4),
@@ -79,69 +83,114 @@ def tile_list_antisymmetric_pair_kernel(tc, xt_words, xt_scales, wa_words, wa_sc
                 stop=True,
             )
 
-        def round_b(c):
+        def round_b(h):
             nc.vector.tensor_copy(
-                out=b_grouped[c][:].rearrange("p (c i) j -> p c j i", i=4),
-                in_=b_raw[c][:].rearrange("p j (c i) -> p c j i", i=4),
+                out=b_grouped[h][:].rearrange("p (c i) j -> p c j i", i=4),
+                in_=b_raw[h][:].rearrange("p j (c i) -> p c j i", i=4),
             )
 
-        def quantise_b(c):
+        def quantise_b(h):
             nc.vector.quantize_mx(
-                out=b_codes[c][:].bitcast(FP8X4),
-                scales=b_scale[c][:],
-                in_=b_grouped[c][:].rearrange("p n j -> p (n j)"),
+                out=b_codes[h][:].bitcast(FP8X4),
+                scales=b_scale[h][:],
+                in_=b_grouped[h][:].rearrange("p n j -> p (n j)"),
             )
 
-        def multiply_b(c):
+        def multiply_b(h, c, after=None):
+            cols = slice(P * (c - WB_LOADS[h][0]), P * (c - WB_LOADS[h][0] + 1))
+            b_bank[c] = psum.tile([P, T], F32, name="b_bank%d" % c, tag=after or "b_bank%d" % c)
             nc.tensor.matmul_mx(
                 out=b_bank[c][:],
-                lhsT=b_codes[c][:].bitcast(FP8X4),
-                lhsT_scale=b_scale[c][:],
+                lhsT=b_codes[h][:, cols].bitcast(FP8X4),
+                lhsT_scale=b_scale[h][:, cols],
                 rhs=x_codes[:].bitcast(FP8X4),
                 rhs_scale=x_scale[:],
                 start=True,
                 stop=True,
             )
 
-        def empty_banks(c):
-            nc.scalar.copy(out=za[c][:, 0:T], in_=a_bank[c][:])
-            if c < VECTOR_EMPTIES:
-                nc.vector.tensor_copy(out=zb[c][:, 0:T], in_=b_bank[c][:])
+        def empty_a(c, copy, after=None):
+            za[c] = sbuf([P, T + SPARE], F32, "za%d" % c, after)
+            copy(out=za[c][:, 0:T], in_=a_bank[c][:])
+
+        def empty_b(c, after=None):
+            zb[c] = sbuf([P, T + SPARE], F32, "zb%d" % c, after)
+            nc.scalar.copy(out=zb[c][:, 0:T], in_=b_bank[c][:])
+
+        def entries(offsets, cols):
+            return offsets[:, cols.start // 16 : cols.stop // 16]
+
+        def pick_b(c, offsets, cols, name):
+            picked = sbuf([P, cols.stop - cols.start], F32, name)
+            nc.scalar.activation(picked[:], zb[c][:].indirect(entries(offsets, cols)), COPY)
+            return picked
+
+        def pick_a_times(product, c, offsets, cols, picked):
+            nc.vector.tensor_tensor(product[c][:, cols], za[c][:].indirect(entries(offsets, cols)), picked[:], MULT)
+
+        def finish(c, cols):
+            nc.vector.tensor_tensor(result[c][:, cols], direct[c][:, cols], swapped[c][:, cols], SUBTRACT)
+            nc.sync.dma_start(out=out[P * c : P * (c + 1), cols], in_=result[c][:, cols])
+
+        def block_tiles(c, direct_after=None, swapped_after=None):
+            direct[c] = sbuf([P, J], F32, "direct%d" % c, direct_after)
+            swapped[c] = sbuf([P, J], F32, "swapped%d" % c, swapped_after)
+            result[c] = sbuf([P, J], F32, "result%d" % c)
+
+        round_b(0)
+        quantise_b(0)
+        multiply_b(0, 0)
+        multiply_a(0)
+        multiply_a(1)
+        empty_b(0)
+        empty_a(0, nc.vector.tensor_copy)
+        round_b(1)
+        quantise_b(1)
+        multiply_b(1, 1, after="a_bank0")
+
+        head = [slice(0, HEAD_CUT), slice(HEAD_CUT, J)]
+        b_second = [pick_b(0, second, cols, "b_second0_%d" % u) for u, cols in enumerate(head)]
+        b_first = pick_b(0, first, ALL, "b_first0")
+        round_b(2)
+        block_tiles(0, swapped_after="b_raw2")
+        for cols, picked in zip(head, b_second):
+            pick_a_times(direct, 0, first, cols, picked)
+        pick_a_times(swapped, 0, second, ALL, b_first)
+        quantise_b(2)
+        multiply_b(2, 2)
+
+        empty_b(1, after="b_second0_0")
+        empty_a(1, nc.vector.tensor_copy)
+        b_second = pick_b(1, second, ALL, "b_second1")
+        b_first = pick_b(1, first, ALL, "b_first1")
+        block_tiles(1, direct_after="b_grouped2", swapped_after="b_first0")
+        pick_a_times(direct, 1, first, ALL, b_second)
+        finish(0, ALL)
+        pick_a_times(swapped, 1, second, ALL, b_first)
+
+        multiply_a(2)
+        empty_b(2)
+        multiply_b(2, 3, after="b_bank2")
+        empty_a(2, nc.scalar.copy, after="direct0")
+        b_second = pick_b(2, second, ALL, "b_second2")
+        b_first = pick_b(2, first, ALL, "b_first2")
+        block_tiles(2)
+        pick_a_times(direct, 2, first, ALL, b_second)
+        finish(1, ALL)
+        pick_a_times(swapped, 2, second, ALL, b_first)
+
+        multiply_a(3)
+        empty_b(3)
+        empty_a(3, nc.scalar.copy, after="b_grouped2")
+        block_tiles(3)
+        tail = [slice(0, TAIL_CUT), slice(TAIL_CUT, J)]
+        for u, cols in enumerate(tail):
+            b_second = pick_b(3, second, cols, "b_second3_%d" % u)
+            b_first = pick_b(3, first, cols, "b_first3_%d" % u)
+            pick_a_times(direct, 3, first, cols, b_second)
+            if u == 0:
+                finish(2, ALL)
             else:
-                nc.scalar.copy(out=zb[c][:, 0:T], in_=b_bank[c][:])
-
-        def products(u):
-            c, lo, hi = PIECES[u]
-            width = hi - lo
-            first_part, second_part = first[:, lo // 16 : hi // 16], second[:, lo // 16 : hi // 16]
-            za_first = keep.tile([P, width], F32, name="za_first%d" % u)
-            za_second = keep.tile([P, width], F32, name="za_second%d" % u)
-            direct = keep.tile([P, width], F32, name="direct%d" % u)
-            swapped = keep.tile([P, width], F32, name="swapped%d" % u)
-            nc.scalar.activation(za_first[:], za[c][:].indirect(first_part), COPY)
-            nc.scalar.activation(za_second[:], za[c][:].indirect(second_part), COPY)
-            nc.vector.tensor_tensor(direct[:], zb[c][:].indirect(second_part), za_first[:], MULT)
-            if u > 0:
-                finish(u - 1)
-            nc.vector.tensor_tensor(swapped[:], zb[c][:].indirect(first_part), za_second[:], MULT)
-            made.append((direct, swapped))
-
-        def finish(u):
-            c, lo, hi = PIECES[u]
-            direct, swapped = made[u]
-            result = keep.tile([P, hi - lo], F32, name="result%d" % u)
-            nc.vector.tensor_tensor(result[:], direct[:], swapped[:], SUBTRACT)
-            nc.sync.dma_start(out=out[P * c : P * (c + 1), lo:hi], in_=result[:])
-
-        made = []
-        for c in range(BLOCKS):
-            round_b(c)
-            quantise_b(c)
-            multiply_a(c)
-            multiply_b(c)
-        for c in range(BLOCKS):
-            empty_banks(c)
-            for u in range(len(PIECES)):
-                if PIECES[u][0] == c:
-                    products(u)
-        finish(len(PIECES) - 1)
+                finish(3, tail[0])
+            pick_a_times(swapped, 3, second, cols, b_first)
+        finish(3, tail[1])

@@ -19,11 +19,12 @@ SUBTRACT = mybir.AluOpType.subtract
 
 P = 128
 PACK = 4
-BLOCKS = N // P
+QUADRANTS = 4
+PER_COLUMN = 16
+RUN = 4
 SPARE = 16
 WB_LOADS = [(0, 1), (1, 2), (2, 4)]
-HEAD_CUT = 256
-TAIL_CUT = 320
+TAIL_START = 352
 ALL = slice(0, J)
 
 
@@ -34,163 +35,162 @@ def tile_list_antisymmetric_pair_kernel(tc, xt_words, xt_scales, wa_words, wa_sc
         keep = ctx.enter_context(tc.tile_pool(name="keep", bufs=1))
         psum = ctx.enter_context(tc.psum_pool(name="psum", bufs=1))
 
-        def sbuf(shape, dtype, name, after=None):
-            return keep.tile(shape, dtype, name=name, tag=after or name, align_bytes=64)
+        def sbuf(shape, dtype, name, reuse=None):
+            return keep.tile(shape, dtype, name=name, tag=reuse or name, align_bytes=64)
 
-        first = lists.tile([P, J // 16], U16, name="first")
-        second = lists.tile([P, J // 16], U16, name="second")
+        def bank(name, reuse=None):
+            return psum.tile([P, T], F32, name=name, tag=reuse or name)
+
+        idx = lists.tile([P, J // PER_COLUMN], U16, name="idx")
+        idx2 = lists.tile([P, J // PER_COLUMN], U16, name="idx2")
         x_codes = sbuf([P, T], U32, "x_codes")
         x_scale = sbuf([P, T], U8, "x_scale")
         a_codes = sbuf([P, 2 * N], U8, "a_codes")
         a_scale = sbuf([P, N], U8, "a_scale")
         widths = [P * (hi - lo) for lo, hi in WB_LOADS]
         b_raw = [sbuf([P, PACK, w], F32, "b_raw%d" % h) for h, w in enumerate(widths)]
-        b_grouped = [sbuf([P, w, PACK], BF16, "b_grouped%d" % h) for h, w in enumerate(widths)]
+        b_rounded = [sbuf([P, w, PACK], BF16, "b_rounded%d" % h) for h, w in enumerate(widths)]
         b_codes = [sbuf([P, w], U32, "b_codes%d" % h) for h, w in enumerate(widths)]
         b_scale = [sbuf([P, w], U8, "b_scale%d" % h) for h, w in enumerate(widths)]
 
-        def load_scales(plane, rows):
-            for q in range(4):
-                nc.sync.dma_start(out=plane[32 * q : 32 * q + 4, :].bitcast(I32), in_=rows[0, 4 * q : 4 * q + 4, :].bitcast(I32))
-
-        wb_rows = wb.rearrange("(p j) n -> p j n", j=PACK)
+        def load_scales(scale, rows):
+            for q in range(QUADRANTS):
+                nc.sync.dma_start(
+                    out=scale[32 * q : 32 * q + 4, :].bitcast(I32),
+                    in_=rows[0, 4 * q : 4 * q + 4, :].bitcast(I32),
+                )
 
         def load_wb(h):
             lo, hi = WB_LOADS[h]
-            nc.sync.dma_start(out=b_raw[h][:], in_=wb_rows[:, :, P * lo : P * hi])
+            rows = wb.rearrange("(p r) n -> p r n", r=PACK)
+            nc.sync.dma_start(out=b_raw[h][:], in_=rows[:, :, P * lo : P * hi])
 
-        load_scales(x_scale, xt_scales)
         load_wb(0)
+        load_scales(x_scale, xt_scales)
         nc.sync.dma_start(out=x_codes[:].bitcast(I32), in_=xt_words[0].rearrange("p t r -> p (t r)").bitcast(I32))
         nc.sync.dma_start(out=a_codes[:].bitcast(I32), in_=wa_words[0].bitcast(I32))
         load_wb(1)
+        nc.sync.dma_start(idx2[:], offs2)
         load_scales(a_scale, wa_scales)
-        nc.sync.dma_start(second[:], offs2)
-        nc.sync.dma_start(first[:], offs)
+        nc.sync.dma_start(idx[:], offs)
         load_wb(2)
 
-        a_bank, b_bank, za, zb, direct, swapped, result = {}, {}, {}, {}, {}, {}, {}
-
-        def multiply_a(c):
-            a_bank[c] = psum.tile([P, T], F32, name="a_bank%d" % c)
-            nc.tensor.matmul_mx(
-                out=a_bank[c][:],
-                lhsT=a_codes[:, 2 * P * c : 2 * P * (c + 1)].bitcast(FP4X4),
-                lhsT_scale=a_scale[:, P * c : P * (c + 1)],
-                rhs=x_codes[:].bitcast(FP8X4),
-                rhs_scale=x_scale[:],
-                start=True,
-                stop=True,
-            )
-
-        def round_b(h):
+        def round_wb(h):
             nc.vector.tensor_copy(
-                out=b_grouped[h][:].rearrange("p (c i) j -> p c j i", i=4),
-                in_=b_raw[h][:].rearrange("p j (c i) -> p c j i", i=4),
+                out=b_rounded[h][:].rearrange("p (c i) r -> p c r i", i=RUN),
+                in_=b_raw[h][:].rearrange("p r (c i) -> p c r i", i=RUN),
             )
 
-        def quantise_b(h):
+        def quantise_wb(h):
             nc.vector.quantize_mx(
                 out=b_codes[h][:].bitcast(FP8X4),
                 scales=b_scale[h][:],
-                in_=b_grouped[h][:].rearrange("p n j -> p (n j)"),
+                in_=b_rounded[h][:].rearrange("p n r -> p (n r)"),
             )
 
-        def multiply_b(h, c, after=None):
-            cols = slice(P * (c - WB_LOADS[h][0]), P * (c - WB_LOADS[h][0] + 1))
-            b_bank[c] = psum.tile([P, T], F32, name="b_bank%d" % c, tag=after or "b_bank%d" % c)
+        def times_xt(acc, codes, scale):
             nc.tensor.matmul_mx(
-                out=b_bank[c][:],
-                lhsT=b_codes[h][:, cols].bitcast(FP8X4),
-                lhsT_scale=b_scale[h][:, cols],
+                out=acc[:],
+                lhsT=codes,
+                lhsT_scale=scale,
                 rhs=x_codes[:].bitcast(FP8X4),
                 rhs_scale=x_scale[:],
                 start=True,
                 stop=True,
             )
+            return acc
 
-        def empty_a(c, copy, after=None):
-            za[c] = sbuf([P, T + SPARE], F32, "za%d" % c, after)
-            copy(out=za[c][:, 0:T], in_=a_bank[c][:])
+        def multiply_a(g, reuse=None):
+            codes = a_codes[:, 2 * P * g : 2 * P * (g + 1)].bitcast(FP4X4)
+            return times_xt(bank("a_bank%d" % g, reuse), codes, a_scale[:, P * g : P * (g + 1)])
 
-        def empty_b(c, after=None):
-            zb[c] = sbuf([P, T + SPARE], F32, "zb%d" % c, after)
-            nc.scalar.copy(out=zb[c][:, 0:T], in_=b_bank[c][:])
+        def multiply_b(g, h, reuse=None):
+            cols = slice(P * (g - WB_LOADS[h][0]), P * (g - WB_LOADS[h][0] + 1))
+            return times_xt(bank("b_bank%d" % g, reuse), b_codes[h][:, cols].bitcast(FP8X4), b_scale[h][:, cols])
 
-        def entries(offsets, cols):
-            return offsets[:, cols.start // 16 : cols.stop // 16]
+        def empty(acc, copy, name, reuse=None):
+            z = sbuf([P, T + SPARE], F32, name, reuse)
+            copy(out=z[:, 0:T], in_=acc[:])
+            return z
 
-        def pick_b(c, offsets, cols, name):
-            picked = sbuf([P, cols.stop - cols.start], F32, name)
-            nc.scalar.activation(picked[:], zb[c][:].indirect(entries(offsets, cols)), COPY)
+        def window(z, entries, pairs):
+            return z[:].indirect(entries[:, pairs.start // PER_COLUMN : pairs.stop // PER_COLUMN])
+
+        def gather(z, entries, pairs, name):
+            picked = sbuf([P, pairs.stop - pairs.start], F32, name)
+            nc.scalar.activation(picked[:], window(z, entries, pairs), COPY)
             return picked
 
-        def pick_a_times(product, c, offsets, cols, picked):
-            nc.vector.tensor_tensor(product[c][:, cols], za[c][:].indirect(entries(offsets, cols)), picked[:], MULT)
+        def gather_times(product, z, entries, pairs, picked):
+            nc.vector.tensor_tensor(product[:, pairs], window(z, entries, pairs), picked[:], MULT)
 
-        def finish(c, cols):
-            nc.vector.tensor_tensor(result[c][:, cols], direct[c][:, cols], swapped[c][:, cols], SUBTRACT)
-            nc.sync.dma_start(out=out[P * c : P * (c + 1), cols], in_=result[c][:, cols])
+        def subtract_and_store(g, direct, swapped, result, pairs):
+            nc.vector.tensor_tensor(result[:, pairs], direct[:, pairs], swapped[:, pairs], SUBTRACT)
+            nc.sync.dma_start(out=out[P * g : P * (g + 1), pairs], in_=result[:, pairs])
 
-        def block_tiles(c, direct_after=None, swapped_after=None):
-            direct[c] = sbuf([P, J], F32, "direct%d" % c, direct_after)
-            swapped[c] = sbuf([P, J], F32, "swapped%d" % c, swapped_after)
-            result[c] = sbuf([P, J], F32, "result%d" % c)
+        def product_tiles(g, direct_reuses=None, swapped_reuses=None):
+            direct = sbuf([P, J], F32, "direct%d" % g, direct_reuses)
+            swapped = sbuf([P, J], F32, "swapped%d" % g, swapped_reuses)
+            return direct, swapped, sbuf([P, J], F32, "result%d" % g)
 
-        round_b(0)
-        quantise_b(0)
-        multiply_b(0, 0)
-        multiply_a(0)
-        multiply_a(1)
-        empty_b(0)
-        empty_a(0, nc.vector.tensor_copy)
-        round_b(1)
-        quantise_b(1)
-        multiply_b(1, 1, after="a_bank0")
+        round_wb(0)
+        quantise_wb(0)
+        b_acc = multiply_b(0, 0)
+        a_acc = multiply_a(0)
+        a_acc_next = multiply_a(1)
+        zb = empty(b_acc, nc.scalar.copy, "zb0")
+        za = empty(a_acc, nc.vector.tensor_copy, "za0")
+        round_wb(1)
+        quantise_wb(1)
+        b_acc_next = multiply_b(1, 1, reuse="a_bank0")
+        zb_idx2 = gather(zb, idx2, ALL, "zb_idx2_0")
+        zb_idx = gather(zb, idx, ALL, "zb_idx_0")
+        products = product_tiles(0, swapped_reuses="b_raw2")
+        gather_times(products[0], za, idx, ALL, zb_idx2)
+        round_wb(2)
+        gather_times(products[1], za, idx2, ALL, zb_idx)
+        quantise_wb(2)
+        b_acc_later = multiply_b(2, 2)
 
-        head = [slice(0, HEAD_CUT), slice(HEAD_CUT, J)]
-        b_second = [pick_b(0, second, cols, "b_second0_%d" % u) for u, cols in enumerate(head)]
-        b_first = pick_b(0, first, ALL, "b_first0")
-        round_b(2)
-        block_tiles(0, swapped_after="b_raw2")
-        for cols, picked in zip(head, b_second):
-            pick_a_times(direct, 0, first, cols, picked)
-        pick_a_times(swapped, 0, second, ALL, b_first)
-        quantise_b(2)
-        multiply_b(2, 2)
+        zb = empty(b_acc_next, nc.scalar.copy, "zb1")
+        za = empty(a_acc_next, nc.scalar.copy, "za1")
+        zb_idx2 = gather(zb, idx2, ALL, "zb_idx2_1")
+        zb_idx = gather(zb, idx, ALL, "zb_idx_1")
+        done = products
+        products = product_tiles(1, direct_reuses="b_rounded2", swapped_reuses="zb_idx_0")
+        gather_times(products[0], za, idx, ALL, zb_idx2)
+        subtract_and_store(0, *done, ALL)
+        gather_times(products[1], za, idx2, ALL, zb_idx)
 
-        empty_b(1, after="b_second0_0")
-        empty_a(1, nc.vector.tensor_copy)
-        b_second = pick_b(1, second, ALL, "b_second1")
-        b_first = pick_b(1, first, ALL, "b_first1")
-        block_tiles(1, direct_after="b_grouped2", swapped_after="b_first0")
-        pick_a_times(direct, 1, first, ALL, b_second)
-        finish(0, ALL)
-        pick_a_times(swapped, 1, second, ALL, b_first)
+        a_acc = multiply_a(2, reuse="a_bank1")
+        zb = empty(b_acc_later, nc.scalar.copy, "zb2")
+        b_acc_next = multiply_b(3, 2, reuse="b_bank2")
+        za = empty(a_acc, nc.scalar.copy, "za2", reuse="direct0")
+        zb_idx2 = gather(zb, idx2, ALL, "zb_idx2_2")
+        zb_idx = gather(zb, idx, ALL, "zb_idx_2")
+        done = products
+        products = product_tiles(2)
+        gather_times(products[0], za, idx, ALL, zb_idx2)
+        subtract_and_store(1, *done, ALL)
+        gather_times(products[1], za, idx2, ALL, zb_idx)
 
-        multiply_a(2)
-        empty_b(2)
-        multiply_b(2, 3, after="b_bank2")
-        empty_a(2, nc.scalar.copy, after="direct0")
-        b_second = pick_b(2, second, ALL, "b_second2")
-        b_first = pick_b(2, first, ALL, "b_first2")
-        block_tiles(2)
-        pick_a_times(direct, 2, first, ALL, b_second)
-        finish(1, ALL)
-        pick_a_times(swapped, 2, second, ALL, b_first)
+        body, tail = slice(0, TAIL_START), slice(TAIL_START, J)
+        a_acc = multiply_a(3, reuse="a_bank1")
+        zb = empty(b_acc_next, nc.scalar.copy, "zb3")
+        za = empty(a_acc, nc.scalar.copy, "za3", reuse="b_rounded2")
+        zb_idx2 = gather(zb, idx2, body, "zb_idx2_3")
+        zb_idx = gather(zb, idx, body, "zb_idx_3")
+        done = products
+        direct, swapped, result = product_tiles(3)
+        gather_times(direct, za, idx, body, zb_idx2)
+        subtract_and_store(2, *done, ALL)
+        gather_times(swapped, za, idx2, body, zb_idx)
 
-        multiply_a(3)
-        empty_b(3)
-        empty_a(3, nc.scalar.copy, after="b_grouped2")
-        block_tiles(3)
-        tail = [slice(0, TAIL_CUT), slice(TAIL_CUT, J)]
-        for u, cols in enumerate(tail):
-            b_second = pick_b(3, second, cols, "b_second3_%d" % u)
-            b_first = pick_b(3, first, cols, "b_first3_%d" % u)
-            pick_a_times(direct, 3, first, cols, b_second)
-            if u == 0:
-                finish(2, ALL)
-            else:
-                finish(3, tail[0])
-            pick_a_times(swapped, 3, second, cols, b_first)
-        finish(3, tail[1])
+        zb_idx2 = gather(zb, idx2, tail, "zb_idx2_tail")
+        za_idx = gather(za, idx, tail, "za_idx_tail")
+        zb_idx = gather(zb, idx, tail, "zb_idx_tail")
+        za_idx2 = gather(za, idx2, tail, "za_idx2_tail")
+        nc.vector.tensor_tensor(direct[:, tail], za_idx[:], zb_idx2[:], MULT)
+        subtract_and_store(3, direct, swapped, result, body)
+        nc.vector.tensor_tensor(swapped[:, tail], za_idx2[:], zb_idx[:], MULT)
+        subtract_and_store(3, direct, swapped, result, tail)

@@ -26,6 +26,8 @@ SPARE = 16
 WB_LOADS = [(0, 1), (1, 2), (2, 4)]
 TAIL_START = 352
 ALL = slice(0, J)
+WHOLE = [slice(0, T)]
+HALVES = [slice(0, T // 2), slice(T // 2, T)]
 
 
 def tile_list_antisymmetric_pair_kernel(tc, xt_words, xt_scales, wa_words, wa_scales, wb, offs, offs2, out):
@@ -38,8 +40,8 @@ def tile_list_antisymmetric_pair_kernel(tc, xt_words, xt_scales, wa_words, wa_sc
         def sbuf(shape, dtype, name, reuse=None):
             return keep.tile(shape, dtype, name=name, tag=reuse or name, align_bytes=64)
 
-        def bank(name, reuse=None):
-            return psum.tile([P, T], F32, name=name, tag=reuse or name)
+        def bank(name, tokens, reuse=None):
+            return psum.tile([P, tokens.stop - tokens.start], F32, name=name, tag=reuse or name)
 
         idx = lists.tile([P, J // PER_COLUMN], U16, name="idx")
         idx2 = lists.tile([P, J // PER_COLUMN], U16, name="idx2")
@@ -53,9 +55,9 @@ def tile_list_antisymmetric_pair_kernel(tc, xt_words, xt_scales, wa_words, wa_sc
         b_codes = [sbuf([P, w], U32, "b_codes%d" % h) for h, w in enumerate(widths)]
         b_scale = [sbuf([P, w], U8, "b_scale%d" % h) for h, w in enumerate(widths)]
 
-        def load_scales(scale, rows):
-            for q in range(QUADRANTS):
-                nc.sync.dma_start(
+        def load_scales(scale, rows, queues):
+            for q, queue in enumerate(queues):
+                queue.dma_start(
                     out=scale[32 * q : 32 * q + 4, :].bitcast(I32),
                     in_=rows[0, 4 * q : 4 * q + 4, :].bitcast(I32),
                 )
@@ -66,12 +68,12 @@ def tile_list_antisymmetric_pair_kernel(tc, xt_words, xt_scales, wa_words, wa_sc
             nc.sync.dma_start(out=b_raw[h][:], in_=rows[:, :, P * lo : P * hi])
 
         load_wb(0)
-        load_scales(x_scale, xt_scales)
+        load_scales(x_scale, xt_scales, [nc.sync] * QUADRANTS)
         nc.sync.dma_start(out=x_codes[:].bitcast(I32), in_=xt_words[0].rearrange("p t r -> p (t r)").bitcast(I32))
         nc.sync.dma_start(out=a_codes[:].bitcast(I32), in_=wa_words[0].bitcast(I32))
         load_wb(1)
         nc.sync.dma_start(idx2[:], offs2)
-        load_scales(a_scale, wa_scales)
+        load_scales(a_scale, wa_scales, [nc.gpsimd] + [nc.sync] * (QUADRANTS - 1))
         nc.sync.dma_start(idx[:], offs)
         load_wb(2)
 
@@ -88,29 +90,34 @@ def tile_list_antisymmetric_pair_kernel(tc, xt_words, xt_scales, wa_words, wa_sc
                 in_=b_rounded[h][:].rearrange("p n r -> p (n r)"),
             )
 
-        def times_xt(acc, codes, scale):
-            nc.tensor.matmul_mx(
-                out=acc[:],
-                lhsT=codes,
-                lhsT_scale=scale,
-                rhs=x_codes[:].bitcast(FP8X4),
-                rhs_scale=x_scale[:],
-                start=True,
-                stop=True,
-            )
-            return acc
+        def times_xt(name, codes, scale, parts, reuse):
+            banks = []
+            for tokens in parts:
+                acc = bank("%s_%d" % (name, tokens.start), tokens, reuse)
+                nc.tensor.matmul_mx(
+                    out=acc[:],
+                    lhsT=codes,
+                    lhsT_scale=scale,
+                    rhs=x_codes[:, tokens].bitcast(FP8X4),
+                    rhs_scale=x_scale[:, tokens],
+                    start=True,
+                    stop=True,
+                )
+                banks.append((tokens, acc))
+            return banks
 
-        def multiply_a(g, reuse=None):
+        def multiply_a(g, parts=WHOLE, reuse=None):
             codes = a_codes[:, 2 * P * g : 2 * P * (g + 1)].bitcast(FP4X4)
-            return times_xt(bank("a_bank%d" % g, reuse), codes, a_scale[:, P * g : P * (g + 1)])
+            return times_xt("a_bank%d" % g, codes, a_scale[:, P * g : P * (g + 1)], parts, reuse)
 
-        def multiply_b(g, h, reuse=None):
+        def multiply_b(g, h, parts=WHOLE, reuse=None):
             cols = slice(P * (g - WB_LOADS[h][0]), P * (g - WB_LOADS[h][0] + 1))
-            return times_xt(bank("b_bank%d" % g, reuse), b_codes[h][:, cols].bitcast(FP8X4), b_scale[h][:, cols])
+            return times_xt("b_bank%d" % g, b_codes[h][:, cols].bitcast(FP8X4), b_scale[h][:, cols], parts, reuse)
 
-        def empty(acc, copy, name, reuse=None):
+        def empty(banks, copy, name, reuse=None):
             z = sbuf([P, T + SPARE], F32, name, reuse)
-            copy(out=z[:, 0:T], in_=acc[:])
+            for tokens, acc in banks:
+                copy(out=z[:, tokens], in_=acc[:])
             return z
 
         def window(z, entries, pairs):
@@ -135,14 +142,14 @@ def tile_list_antisymmetric_pair_kernel(tc, xt_words, xt_scales, wa_words, wa_sc
 
         round_wb(0)
         quantise_wb(0)
-        b_acc = multiply_b(0, 0)
-        a_acc = multiply_a(0)
+        b_acc = multiply_b(0, 0, HALVES)
+        a_acc = multiply_a(0, HALVES)
         a_acc_next = multiply_a(1)
         zb = empty(b_acc, nc.scalar.copy, "zb0")
         za = empty(a_acc, nc.vector.tensor_copy, "za0")
         round_wb(1)
         quantise_wb(1)
-        b_acc_next = multiply_b(1, 1, reuse="a_bank0")
+        b_acc_next = multiply_b(1, 1, reuse="a_bank0_0")
         zb_idx2 = gather(zb, idx2, ALL, "zb_idx2_0")
         zb_idx = gather(zb, idx, ALL, "zb_idx_0")
         products = product_tiles(0, swapped_reuses="b_raw2")
@@ -162,9 +169,9 @@ def tile_list_antisymmetric_pair_kernel(tc, xt_words, xt_scales, wa_words, wa_sc
         subtract_and_store(0, *done, ALL)
         gather_times(products[1], za, idx2, ALL, zb_idx)
 
-        a_acc = multiply_a(2, reuse="a_bank1")
+        a_acc = multiply_a(2, reuse="a_bank1_0")
         zb = empty(b_acc_later, nc.scalar.copy, "zb2")
-        b_acc_next = multiply_b(3, 2, reuse="b_bank2")
+        b_acc_next = multiply_b(3, 2, reuse="b_bank2_0")
         za = empty(a_acc, nc.scalar.copy, "za2", reuse="direct0")
         zb_idx2 = gather(zb, idx2, ALL, "zb_idx2_2")
         zb_idx = gather(zb, idx, ALL, "zb_idx_2")
@@ -175,7 +182,7 @@ def tile_list_antisymmetric_pair_kernel(tc, xt_words, xt_scales, wa_words, wa_sc
         gather_times(products[1], za, idx2, ALL, zb_idx)
 
         body, tail = slice(0, TAIL_START), slice(TAIL_START, J)
-        a_acc = multiply_a(3, reuse="a_bank1")
+        a_acc = multiply_a(3, reuse="a_bank1_0")
         zb = empty(b_acc_next, nc.scalar.copy, "zb3")
         za = empty(a_acc, nc.scalar.copy, "za3", reuse="b_rounded2")
         zb_idx2 = gather(zb, idx2, body, "zb_idx2_3")

from contextlib import ExitStack

import concourse.mybir as mybir

K, T, J, N = 512, 512, 512, 512
FLOPS = 2 * 2 * K * N * T

F32 = mybir.dt.float32
BF16 = mybir.dt.bfloat16
I32 = mybir.dt.int32
U32 = mybir.dt.uint32
U16 = mybir.dt.uint16
U8 = mybir.dt.uint8
FP8X4 = mybir.dt.float8_e4m3fn_x4
FP4X4 = mybir.dt.float4_e2m1fn_x4
COPY = mybir.ActivationFunctionType.Copy
MULT = mybir.AluOpType.mult
SUBTRACT = mybir.AluOpType.subtract

P = 128
PACK = 4
QUADRANTS = 4
PER_COLUMN = 16
RUN = 4
SPARE = 16
WB_LOADS = [(0, 1), (1, 2), (2, 4)]
TAIL_START = 352
ALL = slice(0, J)
WHOLE = [slice(0, T)]
HALVES = [slice(0, T // 2), slice(T // 2, T)]


def tile_list_antisymmetric_pair_kernel(tc, xt_words, xt_scales, wa_words, wa_scales, wb, offs, offs2, out):
    nc = tc.nc
    with ExitStack() as ctx:
        lists = ctx.enter_context(tc.tile_pool(name="lists", bufs=1))
        keep = ctx.enter_context(tc.tile_pool(name="keep", bufs=1))
        psum = ctx.enter_context(tc.psum_pool(name="psum", bufs=1))

        def sbuf(shape, dtype, name, reuse=None):
            return keep.tile(shape, dtype, name=name, tag=reuse or name, align_bytes=64)

        def bank(name, tokens, reuse=None):
            return psum.tile([P, tokens.stop - tokens.start], F32, name=name, tag=reuse or name)

        idx = lists.tile([P, J // PER_COLUMN], U16, name="idx")
        idx2 = lists.tile([P, J // PER_COLUMN], U16, name="idx2")
        x_codes = sbuf([P, T], U32, "x_codes")
        x_scale = sbuf([P, T], U8, "x_scale")
        a_codes = sbuf([P, 2 * N], U8, "a_codes")
        a_scale = sbuf([P, N], U8, "a_scale")
        widths = [P * (hi - lo) for lo, hi in WB_LOADS]
        b_raw = [sbuf([P, PACK, w], F32, "b_raw%d" % h) for h, w in enumerate(widths)]
        b_rounded = [sbuf([P, w, PACK], BF16, "b_rounded%d" % h) for h, w in enumerate(widths)]
        b_codes = [sbuf([P, w], U32, "b_codes%d" % h) for h, w in enumerate(widths)]
        b_scale = [sbuf([P, w], U8, "b_scale%d" % h) for h, w in enumerate(widths)]

        def load_scales(scale, rows, queues):
            for q, queue in enumerate(queues):
                queue.dma_start(
                    out=scale[32 * q : 32 * q + 4, :].bitcast(I32),
                    in_=rows[0, 4 * q : 4 * q + 4, :].bitcast(I32),
                )

        def load_wb(h):
            lo, hi = WB_LOADS[h]
            rows = wb.rearrange("(p r) n -> p r n", r=PACK)
            nc.sync.dma_start(out=b_raw[h][:], in_=rows[:, :, P * lo : P * hi])

        load_wb(0)
        load_scales(x_scale, xt_scales, [nc.sync] * QUADRANTS)
        nc.sync.dma_start(out=x_codes[:].bitcast(I32), in_=xt_words[0].rearrange("p t r -> p (t r)").bitcast(I32))
        nc.sync.dma_start(out=a_codes[:].bitcast(I32), in_=wa_words[0].bitcast(I32))
        load_wb(1)
        nc.sync.dma_start(idx2[:], offs2)
        load_scales(a_scale, wa_scales, [nc.gpsimd] + [nc.sync] * (QUADRANTS - 1))
        nc.sync.dma_start(idx[:], offs)
        load_wb(2)

        def round_wb(h):
            nc.vector.tensor_copy(
                out=b_rounded[h][:].rearrange("p (c i) r -> p c r i", i=RUN),
                in_=b_raw[h][:].rearrange("p r (c i) -> p c r i", i=RUN),
            )

        def quantise_wb(h):
            nc.vector.quantize_mx(
                out=b_codes[h][:].bitcast(FP8X4),
                scales=b_scale[h][:],
                in_=b_rounded[h][:].rearrange("p n r -> p (n r)"),
            )

        def times_xt(name, codes, scale, parts, reuse):
            banks = []
            for tokens in parts:
                acc = bank("%s_%d" % (name, tokens.start), tokens, reuse)
                nc.tensor.matmul_mx(
                    out=acc[:],
                    lhsT=codes,
                    lhsT_scale=scale,
                    rhs=x_codes[:, tokens].bitcast(FP8X4),
                    rhs_scale=x_scale[:, tokens],
                    start=True,
                    stop=True,
                )
                banks.append((tokens, acc))
            return banks

        def multiply_a(g, parts=WHOLE, reuse=None):
            codes = a_codes[:, 2 * P * g : 2 * P * (g + 1)].bitcast(FP4X4)
            return times_xt("a_bank%d" % g, codes, a_scale[:, P * g : P * (g + 1)], parts, reuse)

        def multiply_b(g, h, parts=WHOLE, reuse=None):
            cols = slice(P * (g - WB_LOADS[h][0]), P * (g - WB_LOADS[h][0] + 1))
            return times_xt("b_bank%d" % g, b_codes[h][:, cols].bitcast(FP8X4), b_scale[h][:, cols], parts, reuse)

        def empty(banks, copy, name, reuse=None):
            z = sbuf([P, T + SPARE], F32, name, reuse)
            for tokens, acc in banks:
                copy(out=z[:, tokens], in_=acc[:])
            return z

        def window(z, entries, pairs):
            return z[:].indirect(entries[:, pairs.start // PER_COLUMN : pairs.stop // PER_COLUMN])

        def gather(z, entries, pairs, name):
            picked = sbuf([P, pairs.stop - pairs.start], F32, name)
            nc.scalar.activation(picked[:], window(z, entries, pairs), COPY)
            return picked

        def gather_times(product, z, entries, pairs, picked):
            nc.vector.tensor_tensor(product[:, pairs], window(z, entries, pairs), picked[:], MULT)

        def subtract_and_store(g, direct, swapped, result, pairs):
            nc.vector.tensor_tensor(result[:, pairs], direct[:, pairs], swapped[:, pairs], SUBTRACT)
            nc.sync.dma_start(out=out[P * g : P * (g + 1), pairs], in_=result[:, pairs])

        def product_tiles(g, direct_reuses=None, swapped_reuses=None):
            direct = sbuf([P, J], F32, "direct%d" % g, direct_reuses)
            swapped = sbuf([P, J], F32, "swapped%d" % g, swapped_reuses)
            return direct, swapped, sbuf([P, J], F32, "result%d" % g)

        round_wb(0)
        quantise_wb(0)
        b_acc = multiply_b(0, 0, HALVES)
        a_acc = multiply_a(0, HALVES)
        a_acc_next = multiply_a(1)
        zb = empty(b_acc, nc.scalar.copy, "zb0")
        za = empty(a_acc, nc.vector.tensor_copy, "za0")
        round_wb(1)
        quantise_wb(1)
        b_acc_next = multiply_b(1, 1, reuse="a_bank0_0")
        zb_idx2 = gather(zb, idx2, ALL, "zb_idx2_0")
        zb_idx = gather(zb, idx, ALL, "zb_idx_0")
        products = product_tiles(0, swapped_reuses="b_raw2")
        gather_times(products[0], za, idx, ALL, zb_idx2)
        round_wb(2)
        gather_times(products[1], za, idx2, ALL, zb_idx)
        quantise_wb(2)
        b_acc_later = multiply_b(2, 2)

        zb = empty(b_acc_next, nc.scalar.copy, "zb1")
        za = empty(a_acc_next, nc.scalar.copy, "za1")
        zb_idx2 = gather(zb, idx2, ALL, "zb_idx2_1")
        zb_idx = gather(zb, idx, ALL, "zb_idx_1")
        done = products
        products = product_tiles(1, direct_reuses="b_rounded2", swapped_reuses="zb_idx_0")
        gather_times(products[0], za, idx, ALL, zb_idx2)
        subtract_and_store(0, *done, ALL)
        gather_times(products[1], za, idx2, ALL, zb_idx)

        a_acc = multiply_a(2, reuse="a_bank1_0")
        zb = empty(b_acc_later, nc.scalar.copy, "zb2")
        b_acc_next = multiply_b(3, 2, reuse="b_bank2_0")
        za = empty(a_acc, nc.scalar.copy, "za2", reuse="direct0")
        zb_idx2 = gather(zb, idx2, ALL, "zb_idx2_2")
        zb_idx = gather(zb, idx, ALL, "zb_idx_2")
        done = products
        products = product_tiles(2)
        gather_times(products[0], za, idx, ALL, zb_idx2)
        subtract_and_store(1, *done, ALL)
        gather_times(products[1], za, idx2, ALL, zb_idx)

        body, tail = slice(0, TAIL_START), slice(TAIL_START, J)
        a_acc = multiply_a(3, reuse="a_bank1_0")
        zb = empty(b_acc_next, nc.scalar.copy, "zb3")
        za = empty(a_acc, nc.scalar.copy, "za3", reuse="b_rounded2")
        zb_idx2 = gather(zb, idx2, body, "zb_idx2_3")
        zb_idx = gather(zb, idx, body, "zb_idx_3")
        done = products
        direct, swapped, result = product_tiles(3)
        gather_times(direct, za, idx, body, zb_idx2)
        subtract_and_store(2, *done, ALL)
        gather_times(swapped, za, idx2, body, zb_idx)

        zb_idx2 = gather(zb, idx2, tail, "zb_idx2_tail")
        za_idx = gather(za, idx, tail, "za_idx_tail")
        zb_idx = gather(zb, idx, tail, "zb_idx_tail")
        za_idx2 = gather(za, idx2, tail, "za_idx2_tail")
        nc.vector.tensor_tensor(direct[:, tail], za_idx[:], zb_idx2[:], MULT)
        subtract_and_store(3, direct, swapped, result, body)
        nc.vector.tensor_tensor(swapped[:, tail], za_idx2[:], zb_idx[:], MULT)
        subtract_and_store(3, direct, swapped, result, tail)
